import numpy as np
import ml_dtypes


def mxq(x, axis, fmt="e4m3"):
    dtype, down = {"e4m3": (ml_dtypes.float8_e4m3fn, 7), "e5m2": (ml_dtypes.float8_e5m2, 14)}[fmt]
    v = np.moveaxis(np.asarray(x, np.float32).astype(ml_dtypes.bfloat16).astype(np.float64), axis, -1)
    blocks = v.reshape(v.shape[:-1] + (-1, 32))
    amax = np.abs(blocks).max(-1, keepdims=True)
    byte = np.maximum(np.where(amax > 0, np.frexp(amax)[1] - 1 + 127, 0) - down, 1)
    scale = np.exp2(byte - 127.0)
    codes = (blocks / scale).astype(np.float32).astype(dtype).astype(np.float64)
    return np.moveaxis((codes * scale).reshape(v.shape), -1, axis)


WIDE = False


def mx_kscale(k):
    if not WIDE:
        return np.ones(k)
    levels = np.array([10, -10, 5, -5, 0])
    if k % 512:
        return np.exp2(np.random.permutation(np.resize(levels, k // 32))).repeat(32)
    a = np.empty((k // 512, 16))
    for p in range(k // 512):
        a[p, :8] = np.random.permutation(np.resize(levels, 8))
        for g in range(8):
            far = levels[np.abs(levels - a[p, g]) >= 10]
            a[p, g + 8] = far[np.random.randint(len(far))]
    return np.exp2(a.ravel()).repeat(32)


def f64(x):
    return np.asarray(x).astype(np.float64)


def striped(idx):
    return np.tile(idx.reshape(-1, 16).T, (8, 1)).astype(np.uint16)


def unstriped(offs):
    return offs[:16].T.reshape(-1).astype(np.int64)


def striped8(idx):
    return np.concatenate([x.reshape(-1, 16).T for x in idx]).astype(np.uint16)


def runs(offs, k):
    lists = np.stack([offs[16 * r : 16 * r + 16].T.reshape(-1) for r in range(8)]).astype(np.int64)
    return lists[np.arange(k) % 512 // 64]


def pack_weight(w):
    k, n = w.shape
    w = f64(np.asarray(w, np.float32).astype(ml_dtypes.bfloat16)).reshape(k // 32, 32, n)
    amax = np.abs(w).max(1)
    byte = np.clip(np.where(amax > 0, np.frexp(amax)[1] - 1 + 127 - 7, 1), 1, 254)
    scaled = (w * np.exp2(127.0 - byte)[:, None, :]).reshape(k, n).astype(np.float32)
    words = np.ascontiguousarray(scaled.reshape(k // 512, 128, 4, n).transpose(0, 1, 3, 2)).astype(ml_dtypes.float8_e4m3fn).view(np.uint8)
    return words, np.ascontiguousarray(byte.astype(np.uint8).reshape(k // 512, 16, n))


def unpack_weight(words, scales):
    g, p, n, _ = words.shape
    vals = np.ascontiguousarray(words).view(ml_dtypes.float8_e4m3fn).astype(np.float64) * np.repeat(np.exp2(scales.astype(np.float64) - 127.0), 8, axis=1)[..., None]
    return vals.transpose(0, 1, 3, 2).reshape(g * 512, n)


def sigmoid(v):
    return 1.0 / (1.0 + np.exp(-np.maximum(v, -700.0)))

def planes(y):
    n, m = y.shape
    v = y.astype(np.float32).astype(ml_dtypes.bfloat16).astype(np.float64).reshape(n // 32, 32, m)
    top = np.abs(v).max(1)
    byte = np.clip(np.where(top > 0, np.frexp(top)[1] - 1 + 127 - 7, 1), 1, 254)
    codes = (v * np.exp2(127.0 - byte)[:, None, :]).reshape(n, m).astype(np.float32).astype(ml_dtypes.float8_e4m3fn).view(np.uint8)
    words = codes.reshape(n // 512, 128, 4, m).transpose(0, 1, 3, 2)
    return np.ascontiguousarray(words), np.ascontiguousarray(byte.astype(np.uint8).reshape(n // 512, 16, m))


K, T, S, H, C = 512, 2048, 512, 512, 512


def setup_inputs():
    n = np.random.standard_normal
    s = mx_kscale(K)[:, None]
    packed_xT = pack_weight(n((K, T)) * s)
    packed_w1 = pack_weight(n((K, H)) / np.sqrt(K) / s)
    return {
        "x_words": packed_xT[0],
        "x_scales": packed_xT[1],
        "w1_words": packed_w1[0],
        "w1_scales": packed_w1[1],
        "gs": (np.random.uniform(0.5, 1.5, (K, 1)) / s).astype(np.float32),
        "offs": striped(np.random.permutation(T)[:S]),
        "n1": striped8(np.stack([np.random.permutation(S) for _ in range(8)])),
        "n2": striped8(np.stack([np.random.permutation(S) for _ in range(8)])),
        "ca": striped(np.random.permutation(T)[:C]),
        "cb": striped(np.random.permutation(T)[:C]),
        "n3": striped8(np.stack([np.random.permutation(S) for _ in range(8)])),
        "n4": striped8(np.stack([np.random.permutation(S) for _ in range(8)])),
        "n5": striped8(np.stack([np.random.permutation(S) for _ in range(8)])),
    }


def reference(x_words, x_scales, w1_words, w1_scales, gs, offs, n1, n2, ca, cb, n3, n4, n5):
    x_ca = unpack_weight(x_words, x_scales)[:, unstriped(ca)]
    xq = unpack_weight(x_words, x_scales)[:, unstriped(offs)]
    y = unpack_weight(w1_words, w1_scales).T @ xq
    st = y[np.arange(H)[:, None], runs(n1, H)] - y
    z = f64(gs) * (y * (sigmoid(st[np.arange(H)[:, None], runs(n2, H)])))
    zq = mxq(z, 0, "e4m3")
    a = 0.0625 * (x_ca.T @ zq)
    x_cb = unpack_weight(x_words, x_scales)[:, unstriped(cb)]
    b = 0.0625 * (x_cb.T @ zq)
    out_0 = np.maximum(np.minimum(a - (0.5 * (a[np.arange(C)[:, None], runs(n3, C)])), b[np.arange(C)[:, None], runs(n4, C)]), b[np.arange(C)[:, None], runs(n5, C)])
    return (out_0,) + planes(out_0)

@@ -1,0 +1,213 @@
+from contextlib import ExitStack
+
+import concourse.mybir as mybir
+
+F32 = mybir.dt.float32
+BF16 = mybir.dt.bfloat16
+I32 = mybir.dt.int32
+U32 = mybir.dt.uint32
+U16 = mybir.dt.uint16
+U8 = mybir.dt.uint8
+FP8X4 = mybir.dt.float8_e4m3fn_x4
+ALU = mybir.AluOpType
+ACT = mybir.ActivationFunctionType
+
+P = 128
+PACK = 4
+T = 2048
+S = 512
+HALF = S // 2
+LIST_COLS = S // 16
+FLOPS = 3 * 2 * 512 * 512 * 512
+
+
+def tile_picked_ccmpclampbhopd_none_po_kernel(
+    tc, x_words, x_scales, w1_words, w1_scales, gs, offs, n1, n2, ca, cb, n3, n4, n5, out_0, out_1, out_2
+):
+    nc = tc.nc
+    with ExitStack() as ctx:
+        keep = ctx.enter_context(tc.tile_pool(name="keep", bufs=1))
+        psum = ctx.enter_context(tc.psum_pool(name="psum", bufs=1))
+
+        def load_list(src, name):
+            tile = keep.tile([P, LIST_COLS], U16, name=name)
+            nc.sync.dma_start(tile[:], src)
+            return tile
+
+        def load_scale_rows(queue, tile, src):
+            for q in range(4):
+                queue.dma_start(tile[32 * q : 32 * q + 4, :].bitcast(I32), src[0, 4 * q : 4 * q + 4, :].bitcast(I32))
+
+        def half_cols(h):
+            return slice(h * HALF, (h + 1) * HALF)
+
+        def half_list(h):
+            return slice(h * LIST_COLS // 2, (h + 1) * LIST_COLS // 2)
+
+        xs = keep.tile([P, T], U8, name="xs", align_bytes=64)
+        ws = keep.tile([P, S], U8, name="ws", tag="ws", align_bytes=64)
+        zero = keep.tile([P, 1], F32, name="zero")
+        nc.vector.memset(xs[:].bitcast(I32), 0)
+        nc.vector.memset(ws[:].bitcast(I32), 0)
+        nc.vector.memset(zero[:], 0.0)
+
+        ww = keep.tile([P, S], U32, name="ww", tag="ww", align_bytes=64)
+        nc.sync.dma_start(ww[:].bitcast(I32), w1_words[0].rearrange("p n t -> p (n t)").bitcast(I32))
+        offs_l = load_list(offs, "offs_l")
+        ca_l = load_list(ca, "ca_l")
+        load_scale_rows(nc.sync, xs, x_scales)
+        xw = keep.tile([P, T], U32, name="xw", align_bytes=64)
+        nc.sync.dma_start(xw[:].bitcast(I32), x_words[0].rearrange("p n t -> p (n t)").bitcast(I32))
+        load_scale_rows(nc.sync, ws, w1_scales)
+        n1_l = load_list(n1, "n1_l")
+        gs_t = keep.tile([P, PACK], F32, name="gs_t")
+        nc.sync.dma_start(gs_t[:], gs.rearrange("(p t) o -> p (t o)", t=PACK))
+        cb_l = load_list(cb, "cb_l")
+        n2_l = load_list(n2, "n2_l")
+        n3_l = load_list(n3, "n3_l")
+        n4_l = load_list(n4, "n4_l")
+        n5_l = load_list(n5, "n5_l")
+
+        ya_win = [keep.tile([P, 2 * S], F32, name=f"ya_win{t}") for t in range(PACK)]
+        st_win = [keep.tile([P, 2 * S], F32, name=f"st_win{t}") for t in range(PACK)]
+        b_win = [keep.tile([P, 2 * S], F32, name=f"b_win{t}") for t in range(PACK)]
+        for t in range(PACK):
+            nc.scalar.activation(ya_win[t][:, S:], zero[:].to_broadcast([P, S]), ACT.Sigmoid)
+
+        def deal_bytes(engine, src, name, tag):
+            dealt = keep.tile([P, S], U8, name=name, tag=tag, align_bytes=64)
+            engine.tensor_copy(
+                dealt[:].rearrange("p (t m) -> p t m", t=PACK), src[:].rearrange("p (m t) -> p t m", t=PACK)
+            )
+            return dealt
+
+        xq_s = keep.tile([P, S], U8, name="xq_s", align_bytes=64)
+        nc.vector.tensor_copy(xq_s[:], xs[:].indirect(offs_l[:]))
+        ca_sg = keep.tile([P, S], U8, name="ca_sg", align_bytes=64)
+        nc.vector.tensor_copy(ca_sg[:], xs[:].indirect(ca_l[:]))
+        xq_w = keep.tile([P, S], U32, name="xq_w", align_bytes=64)
+        nc.vector.tensor_copy(xq_w[:], xw[:].indirect(offs_l[:]))
+
+        w_w = keep.tile([P, S], U32, name="w_w", align_bytes=64)
+        nc.vector.tensor_copy(
+            w_w[:].rearrange("p (t m) -> p m t", t=PACK), ww[:].rearrange("p (m t) -> p m t", t=PACK)
+        )
+        w_s = keep.tile([P, S], U8, name="w_s", tag="late_bytes", align_bytes=64)
+        nc.vector.tensor_copy(
+            w_s[:].rearrange("p (t m) -> p t m", t=PACK), ws[:].rearrange("p (m t) -> p t m", t=PACK)
+        )
+
+        ca_w = keep.tile([P, S], U32, name="ca_w", tag="ws", align_bytes=64)
+        nc.vector.tensor_copy(ca_w[:].rearrange("p (t m) -> p m t", t=PACK), xw[:].indirect(ca_l[:]))
+        ca_s = deal_bytes(nc.vector, ca_sg, "ca_s", "ww")
+
+        def product(bank, words, scales, t, rhs, rhs_scale):
+            cols = slice(t * P, (t + 1) * P)
+            nc.tensor.matmul_mx(
+                out=bank,
+                lhsT=words[:, cols].bitcast(FP8X4),
+                lhsT_scale=scales[:, cols],
+                rhs=rhs.bitcast(FP8X4),
+                rhs_scale=rhs_scale,
+                start=True,
+                stop=True,
+            )
+
+        y_bank = [psum.tile([P, S], F32, name=f"y_bank{t}", tag=f"yb{t}") for t in range(PACK)]
+        yg = keep.tile([P, PACK, S], F32, name="yg")
+        sig = keep.tile([P, PACK, S], F32, name="sig")
+        for t in range(PACK):
+            product(y_bank[t][:], w_w, w_s, t, xq_w[:], xq_s[:])
+            nc.scalar.copy(ya_win[t][:, :S], y_bank[t][:])
+            nc.scalar.copy(st_win[t][:, S:], y_bank[t][:])
+            nc.vector.tensor_tensor(st_win[t][:, :S], ya_win[t][:].indirect(n1_l[:]), st_win[t][:, S:], ALU.subtract)
+
+        cb_sg = keep.tile([P, S], U8, name="cb_sg", tag="late_bytes", align_bytes=64)
+        nc.vector.tensor_copy(cb_sg[:], xs[:].indirect(cb_l[:]))
+        cb_s = deal_bytes(nc.vector, cb_sg, "cb_s", "cb_s")
+
+        z_w = keep.tile([P, S], U32, name="z_w", align_bytes=64)
+        z_s = keep.tile([P, S], U8, name="z_s", align_bytes=64)
+        a_bank = [psum.tile([P, S], F32, name=f"a_bank{t}") for t in range(PACK)]
+        for t in range(PACK):
+            nc.vector.tensor_scalar(yg[:, t, :], st_win[t][:, S:], gs_t[:, t : t + 1], None, ALU.mult)
+        for h in range(2):
+            cols = half_cols(h)
+            for t in range(PACK):
+                nc.scalar.activation(sig[:, t, cols], st_win[t][:].indirect(n2_l[:, half_list(h)]), ACT.Sigmoid)
+            z_bf = keep.tile([P, HALF * PACK], BF16, name=f"z_bf{h}", tag=f"z_bf{h}", align_bytes=64)
+            nc.vector.tensor_tensor(
+                z_bf[:].rearrange("p (c i t) -> p c t i", i=4, t=PACK),
+                yg[:, :, cols].rearrange("p t (c i) -> p c t i", i=4),
+                sig[:, :, cols].rearrange("p t (c i) -> p c t i", i=4),
+                ALU.mult,
+            )
+            nc.vector.quantize_mx(z_w[:, cols].bitcast(FP8X4), z_s[:, cols], z_bf[:])
+            product(a_bank[0][:, cols], ca_w, ca_s, 0, z_w[:, cols], z_s[:, cols])
+            nc.scalar.activation(ya_win[0][:, cols], a_bank[0][:, cols], ACT.Copy, scale=-0.03125)
+            nc.scalar.activation(b_win[0][:, S + h * HALF : S + (h + 1) * HALF], a_bank[0][:, cols], ACT.Copy, scale=0.0625)
+
+        cb_w = keep.tile([P, S], U32, name="cb_w", tag="z_bf1", align_bytes=64)
+        nc.vector.tensor_copy(cb_w[:].rearrange("p (t m) -> p m t", t=PACK), xw[:].indirect(cb_l[:]))
+
+        res = keep.tile([P, PACK, S], F32, name="res")
+        out_rows = out_0.rearrange("(p t) s -> p t s", t=PACK)
+        o_w = keep.tile([P, S], U32, name="o_w", align_bytes=64)
+        o_s = keep.tile([P, S], U8, name="o_s", align_bytes=64)
+        o_bf = keep.tile([P, S * PACK], BF16, name="o_bf", align_bytes=64)
+        out_words = out_1[0].rearrange("p n t -> p (n t)").bitcast(I32)
+
+        work = ctx.enter_context(tc.tile_pool(name="work", bufs=2))
+
+        for t in range(PACK):
+            if t > 0:
+                product(a_bank[t][:], ca_w, ca_s, t, z_w[:], z_s[:])
+                nc.scalar.activation(ya_win[t][:, :S], a_bank[t][:], ACT.Copy, scale=-0.03125)
+                nc.scalar.activation(b_win[t][:, S:], a_bank[t][:], ACT.Copy, scale=0.0625)
+            b_bank = psum.tile([P, S], F32, name=f"b_bank{t}", tag=f"yb{t}")
+            product(b_bank[:], cb_w, cb_s, t, z_w[:], z_s[:])
+            nc.scalar.activation(b_win[t][:, :S], b_bank[:], ACT.Copy, scale=0.0625)
+
+        def interleave(copy, cols):
+            copy(
+                o_bf[:, cols.start * PACK : cols.stop * PACK].rearrange("p (c i t) -> p c t i", i=4, t=PACK),
+                res[:, :, cols].rearrange("p t (c i) -> p c t i", i=4),
+            )
+
+        pieces = [(t, slice(0, S), slice(0, LIST_COLS)) for t in range(PACK - 1)]
+        pieces = pieces + [(PACK - 1, half_cols(h), half_list(h)) for h in range(2)]
+        pending = None
+
+        def finish(t, cols, low, b5):
+            nc.vector.tensor_tensor(res[:, t, cols], low, b5, ALU.max)
+            nc.sync.dma_start(out_rows[:, t, cols], res[:, t, cols])
+
+        def planes(cols):
+            nc.vector.quantize_mx(
+                o_w[:, cols].bitcast(FP8X4), o_s[:, cols], o_bf[:, cols.start * PACK : cols.stop * PACK]
+            )
+            nc.sync.dma_start(out_words[:, cols], o_w[:, cols].bitcast(I32))
+
+        for t, cols, lcols in pieces:
+            n = cols.stop - cols.start
+            u = work.tile([P, S], F32, name="u")
+            b4 = work.tile([P, S], F32, name="b4")
+            b5 = work.tile([P, S], F32, name="b5")
+            low = work.tile([P, S], F32, name="low")
+            plain_a = b_win[t][:, S + cols.start : S + cols.stop]
+            nc.vector.tensor_tensor(u[:, :n], ya_win[t][:].indirect(n3_l[:, lcols]), plain_a, ALU.add)
+            nc.vector.tensor_copy(b4[:, :n], b_win[t][:].indirect(n4_l[:, lcols]))
+            if pending is not None:
+                finish(*pending)
+            nc.vector.tensor_copy(b5[:, :n], b_win[t][:].indirect(n5_l[:, lcols]))
+            nc.vector.tensor_tensor(low[:, :n], u[:, :n], b4[:, :n], ALU.min)
+            pending = (t, cols, low[:, :n], b5[:, :n])
+        interleave(nc.scalar.copy, half_cols(0))
+        planes(half_cols(0))
+        finish(*pending)
+        interleave(nc.vector.tensor_copy, slice(HALF, HALF + 160))
+        interleave(nc.scalar.copy, slice(HALF + 160, S))
+        planes(half_cols(1))
+        for q in range(4):
+            queue = nc.scalar if q % 2 else nc.sync
+            queue.dma_start(out_2[0, 4 * q : 4 * q + 4, :].bitcast(I32), o_s[32 * q : 32 * q + 4, :].bitcast(I32))

@@ -1,6 +1,7 @@
 from contextlib import ExitStack
 
 import concourse.mybir as mybir
+from concourse.masks import make_identity
 
 F32 = mybir.dt.float32
 BF16 = mybir.dt.bfloat16
@@ -27,6 +28,7 @@ def tile_picked_ccmpclampbhopd_none_po_kernel(
     nc = tc.nc
     with ExitStack() as ctx:
         keep = ctx.enter_context(tc.tile_pool(name="keep", bufs=1))
+        shared = ctx.enter_context(tc.tile_pool(name="shared", bufs=1))
         psum = ctx.enter_context(tc.psum_pool(name="psum", bufs=1))
 
         def load_list(src, name):
@@ -45,7 +47,7 @@ def tile_picked_ccmpclampbhopd_none_po_kernel(
             return slice(h * LIST_COLS // 2, (h + 1) * LIST_COLS // 2)
 
         xs = keep.tile([P, T], U8, name="xs", align_bytes=64)
-        ws = keep.tile([P, S], U8, name="ws", tag="ws", align_bytes=64)
+        ws = shared.tile([P, S], U8, name="ws", offset=1792, align_bytes=64)
         zero = keep.tile([P, 1], F32, name="zero")
         nc.vector.memset(xs[:].bitcast(I32), 0)
         nc.vector.memset(ws[:].bitcast(I32), 0)
@@ -68,22 +70,22 @@ def tile_picked_ccmpclampbhopd_none_po_kernel(
         n4_l = load_list(n4, "n4_l")
         n5_l = load_list(n5, "n5_l")
 
-        ya_win = [keep.tile([P, 2 * S], F32, name=f"ya_win{t}") for t in range(PACK)]
+        y_win = [keep.tile([P, 2 * S], F32, name=f"y_win{t}", tag=f"y_win{t}", align_bytes=64) for t in range(PACK)]
         st_win = [keep.tile([P, 2 * S], F32, name=f"st_win{t}") for t in range(PACK)]
+        ident = keep.tile([P, P], F32, name="ident")
+        make_identity(nc, ident[:])
         b_win = [keep.tile([P, 2 * S], F32, name=f"b_win{t}") for t in range(PACK)]
         for t in range(PACK):
-            nc.scalar.activation(ya_win[t][:, S:], zero[:].to_broadcast([P, S]), ACT.Sigmoid)
+            nc.scalar.activation(y_win[t][:, S:], zero[:].to_broadcast([P, S]), ACT.Sigmoid)
 
-        def deal_bytes(engine, src, name, tag):
-            dealt = keep.tile([P, S], U8, name=name, tag=tag, align_bytes=64)
-            engine.tensor_copy(
+        def deal_bytes(dealt, src):
+            nc.vector.tensor_copy(
                 dealt[:].rearrange("p (t m) -> p t m", t=PACK), src[:].rearrange("p (m t) -> p t m", t=PACK)
             )
-            return dealt
 
         xq_s = keep.tile([P, S], U8, name="xq_s", align_bytes=64)
         nc.vector.tensor_copy(xq_s[:], xs[:].indirect(offs_l[:]))
-        ca_sg = keep.tile([P, S], U8, name="ca_sg", align_bytes=64)
+        ca_sg = keep.tile([P, S], U8, name="ca_sg", tag="picked_bytes", align_bytes=64)
         nc.vector.tensor_copy(ca_sg[:], xs[:].indirect(ca_l[:]))
         xq_w = keep.tile([P, S], U32, name="xq_w", align_bytes=64)
         nc.vector.tensor_copy(xq_w[:], xw[:].indirect(offs_l[:]))
@@ -92,14 +94,17 @@ def tile_picked_ccmpclampbhopd_none_po_kernel(
         nc.vector.tensor_copy(
             w_w[:].rearrange("p (t m) -> p m t", t=PACK), ww[:].rearrange("p (m t) -> p m t", t=PACK)
         )
-        w_s = keep.tile([P, S], U8, name="w_s", tag="late_bytes", align_bytes=64)
+        w_s = keep.tile([P, S], U8, name="w_s", align_bytes=64)
         nc.vector.tensor_copy(
             w_s[:].rearrange("p (t m) -> p t m", t=PACK), ws[:].rearrange("p (m t) -> p t m", t=PACK)
         )
 
-        ca_w = keep.tile([P, S], U32, name="ca_w", tag="ws", align_bytes=64)
+        ca_w = shared.tile([P, S], U32, name="ca_w", offset=0, align_bytes=64)
         nc.vector.tensor_copy(ca_w[:].rearrange("p (t m) -> p m t", t=PACK), xw[:].indirect(ca_l[:]))
-        ca_s = deal_bytes(nc.vector, ca_sg, "ca_s", "ww")
+        ca_s = shared.tile([P, S], U8, name="ca_s", offset=2048, align_bytes=64)
+        deal_bytes(ca_s, ca_sg)
+        cb_sg = keep.tile([P, S], U8, name="cb_sg", tag="picked_bytes", align_bytes=64)
+        nc.vector.tensor_copy(cb_sg[:], xs[:].indirect(cb_l[:]))
 
         def product(bank, words, scales, t, rhs, rhs_scale):
             cols = slice(t * P, (t + 1) * P)
@@ -114,28 +119,32 @@ def tile_picked_ccmpclampbhopd_none_po_kernel(
             )
 
         y_bank = [psum.tile([P, S], F32, name=f"y_bank{t}", tag=f"yb{t}") for t in range(PACK)]
-        yg = keep.tile([P, PACK, S], F32, name="yg")
         sig = keep.tile([P, PACK, S], F32, name="sig")
         for t in range(PACK):
             product(y_bank[t][:], w_w, w_s, t, xq_w[:], xq_s[:])
-            nc.scalar.copy(ya_win[t][:, :S], y_bank[t][:])
-            nc.scalar.copy(st_win[t][:, S:], y_bank[t][:])
-            nc.vector.tensor_tensor(st_win[t][:, :S], ya_win[t][:].indirect(n1_l[:]), st_win[t][:, S:], ALU.subtract)
+            nc.scalar.copy(y_win[t][:, :S], y_bank[t][:])
+            if t == 0:
+                nc.scalar.copy(st_win[t][:, S:], y_bank[t][:])
+            else:
+                nc.vector.tensor_copy(st_win[t][:, S:], y_win[t][:, :S])
+            nc.vector.tensor_tensor(st_win[t][:, :S], y_win[t][:].indirect(n1_l[:]), st_win[t][:, S:], ALU.subtract)
 
-        cb_sg = keep.tile([P, S], U8, name="cb_sg", tag="late_bytes", align_bytes=64)
-        nc.vector.tensor_copy(cb_sg[:], xs[:].indirect(cb_l[:]))
-        cb_s = deal_bytes(nc.vector, cb_sg, "cb_s", "cb_s")
+        yg = keep.tile([P, PACK, S], F32, name="yg", tag="y_win3", align_bytes=64)
 
         z_w = keep.tile([P, S], U32, name="z_w", align_bytes=64)
         z_s = keep.tile([P, S], U8, name="z_s", align_bytes=64)
-        a_bank = [psum.tile([P, S], F32, name=f"a_bank{t}") for t in range(PACK)]
+        a_bank = [psum.tile([P, S], F32, name=f"a_bank{t}", tag=f"ab{t}") for t in range(PACK)]
+        a_win = y_win[:1] + st_win[1:]
         for t in range(PACK):
             nc.vector.tensor_scalar(yg[:, t, :], st_win[t][:, S:], gs_t[:, t : t + 1], None, ALU.mult)
+        for t in range(2):
+            nc.scalar.activation(sig[:, t, :], st_win[t][:].indirect(n2_l[:]), ACT.Sigmoid)
+        for h in range(2):
+            for t in range(2, PACK):
+                nc.scalar.activation(sig[:, t, half_cols(h)], st_win[t][:].indirect(n2_l[:, half_list(h)]), ACT.Sigmoid)
         for h in range(2):
             cols = half_cols(h)
-            for t in range(PACK):
-                nc.scalar.activation(sig[:, t, cols], st_win[t][:].indirect(n2_l[:, half_list(h)]), ACT.Sigmoid)
-            z_bf = keep.tile([P, HALF * PACK], BF16, name=f"z_bf{h}", tag=f"z_bf{h}", align_bytes=64)
+            z_bf = shared.tile([P, HALF * PACK], BF16, name=f"z_bf{h}", offset=8192 if h == 0 else 4096 + 256, align_bytes=64)
             nc.vector.tensor_tensor(
                 z_bf[:].rearrange("p (c i t) -> p c t i", i=4, t=PACK),
                 yg[:, :, cols].rearrange("p t (c i) -> p c t i", i=4),
@@ -144,11 +153,13 @@ def tile_picked_ccmpclampbhopd_none_po_kernel(
             )
             nc.vector.quantize_mx(z_w[:, cols].bitcast(FP8X4), z_s[:, cols], z_bf[:])
             product(a_bank[0][:, cols], ca_w, ca_s, 0, z_w[:, cols], z_s[:, cols])
-            nc.scalar.activation(ya_win[0][:, cols], a_bank[0][:, cols], ACT.Copy, scale=-0.03125)
+            nc.scalar.activation(a_win[0][:, cols], a_bank[0][:, cols], ACT.Copy, scale=-0.03125)
             nc.scalar.activation(b_win[0][:, S + h * HALF : S + (h + 1) * HALF], a_bank[0][:, cols], ACT.Copy, scale=0.0625)
 
-        cb_w = keep.tile([P, S], U32, name="cb_w", tag="z_bf1", align_bytes=64)
+        cb_w = shared.tile([P, S], U32, name="cb_w", offset=4096 + 512, align_bytes=64)
         nc.vector.tensor_copy(cb_w[:].rearrange("p (t m) -> p m t", t=PACK), xw[:].indirect(cb_l[:]))
+        cb_s = shared.tile([P, S], U8, name="cb_s", offset=4096, align_bytes=64)
+        deal_bytes(cb_s, cb_sg)
 
         res = keep.tile([P, PACK, S], F32, name="res")
         out_rows = out_0.rearrange("(p t) s -> p t s", t=PACK)
@@ -162,7 +173,7 @@ def tile_picked_ccmpclampbhopd_none_po_kernel(
         for t in range(PACK):
             if t > 0:
                 product(a_bank[t][:], ca_w, ca_s, t, z_w[:], z_s[:])
-                nc.scalar.activation(ya_win[t][:, :S], a_bank[t][:], ACT.Copy, scale=-0.03125)
+                nc.scalar.activation(a_win[t][:, :S], a_bank[t][:], ACT.Copy, scale=-0.03125)
                 nc.scalar.activation(b_win[t][:, S:], a_bank[t][:], ACT.Copy, scale=0.0625)
             b_bank = psum.tile([P, S], F32, name=f"b_bank{t}", tag=f"yb{t}")
             product(b_bank[:], cb_w, cb_s, t, z_w[:], z_s[:])
@@ -174,37 +185,100 @@ def tile_picked_ccmpclampbhopd_none_po_kernel(
                 res[:, :, cols].rearrange("p t (c i) -> p c t i", i=4),
             )
 
-        pieces = [(t, slice(0, S), slice(0, LIST_COLS)) for t in range(PACK - 1)]
-        pieces = pieces + [(PACK - 1, half_cols(h), half_list(h)) for h in range(2)]
-        pending = None
-
-        def finish(t, cols, low, b5):
-            nc.vector.tensor_tensor(res[:, t, cols], low, b5, ALU.max)
-            nc.sync.dma_start(out_rows[:, t, cols], res[:, t, cols])
-
         def planes(cols):
             nc.vector.quantize_mx(
                 o_w[:, cols].bitcast(FP8X4), o_s[:, cols], o_bf[:, cols.start * PACK : cols.stop * PACK]
             )
             nc.sync.dma_start(out_words[:, cols], o_w[:, cols].bitcast(I32))
 
-        for t, cols, lcols in pieces:
-            n = cols.stop - cols.start
-            u = work.tile([P, S], F32, name="u")
-            b4 = work.tile([P, S], F32, name="b4")
-            b5 = work.tile([P, S], F32, name="b5")
-            low = work.tile([P, S], F32, name="low")
-            plain_a = b_win[t][:, S + cols.start : S + cols.stop]
-            nc.vector.tensor_tensor(u[:, :n], ya_win[t][:].indirect(n3_l[:, lcols]), plain_a, ALU.add)
-            nc.vector.tensor_copy(b4[:, :n], b_win[t][:].indirect(n4_l[:, lcols]))
-            if pending is not None:
-                finish(*pending)
-            nc.vector.tensor_copy(b5[:, :n], b_win[t][:].indirect(n5_l[:, lcols]))
-            nc.vector.tensor_tensor(low[:, :n], u[:, :n], b4[:, :n], ALU.min)
-            pending = (t, cols, low[:, :n], b5[:, :n])
+        last = PACK - 1
+        u = [None] * PACK
+        d4 = [None] * last
+        d5 = [None] * last
+        turned = {}
+        spans = {0: [slice(0, S)], 1: [slice(0, S)], 2: [half_cols(0), half_cols(1)]}
+
+        def blocks(cols):
+            return [slice(c, c + P) for c in range(cols.start, cols.stop, P)]
+
+        def make_u(t):
+            u[t] = keep.tile([P, S], F32, name=f"u{t}", tag=f"u{t}")
+            nc.vector.tensor_tensor(u[t][:], a_win[t][:].indirect(n3_l[:]), b_win[t][:, S:], ALU.add)
+
+        def turn_u(t):
+            for i, cols in enumerate(spans[t]):
+                turned[t, i] = psum.tile([P, S], F32, name=f"turned{t}_{i}", tag=f"ab{t}" if i == 0 else "ab0")
+                for block in blocks(cols):
+                    nc.tensor.matmul(
+                        turned[t, i][:, block], u[t][:, block], ident[:],
+                        start=block.start == cols.start, stop=False, is_transpose=True,
+                    )
+
+        def make_d4(t):
+            d4[t] = keep.tile([P, S], F32, name=f"d4_{t}", tag=f"u{last}" if t == last - 1 else f"d4_{t}")
+            nc.vector.tensor_tensor(d4[t][:], b_win[t][:].indirect(n4_l[:]), u[t][:], ALU.subtract)
+
+        def make_d5(t):
+            d5[t] = keep.tile([P, S], F32, name=f"d5_{t}")
+            nc.vector.tensor_tensor(d5[t][:], b_win[t][:].indirect(n5_l[:]), u[t][:], ALU.subtract)
+
+        def clamp_and_add(t):
+            w = work.tile([P, S], F32, name="w")
+            nc.vector.scalar_tensor_tensor(w[:], d4[t][:], 0.0, d5[t][:], ALU.min, ALU.max)
+            turn_u(t)
+            turned_sb = work.tile([P, S], F32, name="turned_sb")
+            for i, cols in enumerate(spans[t]):
+                for block in blocks(cols):
+                    nc.tensor.matmul(
+                        turned[t, i][:, block], w[:, block], ident[:],
+                        start=False, stop=block.stop == cols.stop, is_transpose=True,
+                    )
+                nc.scalar.copy(turned_sb[:, cols], turned[t, i][:, cols])
+            for i, cols in enumerate(spans[t]):
+                back = psum.tile([P, S], F32, name=f"back{t}_{i}", tag=f"yb{t}" if i == 0 else "yb0")
+                for block in blocks(cols):
+                    nc.tensor.transpose(back[:, block], turned_sb[:, block], ident[:])
+                nc.scalar.copy(res[:, t, cols], back[:, cols])
+            nc.sync.dma_start(out_rows[:, t, :], res[:, t, :])
+
+        b4 = [keep.tile([P, HALF], F32, name=f"b4_{h}") for h in range(2)]
+        b5 = [keep.tile([P, HALF], F32, name=f"b5_{h}") for h in range(2)]
+        low = [keep.tile([P, HALF], F32, name=f"low{h}") for h in range(2)]
+
+        def fetch_b(dst, lst, h):
+            nc.vector.tensor_copy(dst[h][:], b_win[last][:].indirect(lst[:, half_list(h)]))
+
+        def make_low(h):
+            nc.vector.tensor_tensor(low[h][:], u[last][:, half_cols(h)], b4[h][:], ALU.min)
+
+        def finish(h):
+            cols = half_cols(h)
+            nc.vector.tensor_tensor(res[:, last, cols], low[h][:], b5[h][:], ALU.max)
+            nc.sync.dma_start(out_rows[:, last, cols], res[:, last, cols])
+
+        make_u(0)
+        make_u(1)
+        make_d4(0)
+        make_d5(0)
+        make_u(2)
+        clamp_and_add(0)
+        make_d4(1)
+        make_d5(1)
+        make_d4(2)
+        clamp_and_add(1)
+        make_d5(2)
+        fetch_b(b4, n4_l, 0)
+        clamp_and_add(2)
+        make_u(last)
+        fetch_b(b5, n5_l, 0)
+        make_low(0)
+        fetch_b(b4, n4_l, 1)
+        finish(0)
+        fetch_b(b5, n5_l, 1)
+        make_low(1)
         interleave(nc.scalar.copy, half_cols(0))
         planes(half_cols(0))
-        finish(*pending)
+        finish(1)
         interleave(nc.vector.tensor_copy, slice(HALF, HALF + 160))
         interleave(nc.scalar.copy, slice(HALF + 160, S))
         planes(half_cols(1))

@@ -47,10 +47,11 @@ def tile_picked_ccmpclampbhopd_none_po_kernel(
             return slice(h * LIST_COLS // 2, (h + 1) * LIST_COLS // 2)
 
         xs = keep.tile([P, T], U8, name="xs", align_bytes=64)
-        ws = shared.tile([P, S], U8, name="ws", offset=1792, align_bytes=64)
+        ws_slot = shared.tile([P, 2 * S], U8, name="ws_slot", offset=1984, align_bytes=64)
+        ws = ws_slot[:, :S]
         zero = keep.tile([P, 1], F32, name="zero")
         nc.vector.memset(xs[:].bitcast(I32), 0)
-        nc.vector.memset(ws[:].bitcast(I32), 0)
+        nc.vector.memset(ws.bitcast(I32), 0)
         nc.vector.memset(zero[:], 0.0)
 
         ww = keep.tile([P, S], U32, name="ww", tag="ww", align_bytes=64)
@@ -73,7 +74,8 @@ def tile_picked_ccmpclampbhopd_none_po_kernel(
         y_win = [keep.tile([P, 2 * S], F32, name=f"y_win{t}", tag=f"y_win{t}", align_bytes=64) for t in range(PACK)]
         st_win = [keep.tile([P, 2 * S], F32, name=f"st_win{t}") for t in range(PACK)]
         ident = keep.tile([P, P], F32, name="ident")
-        make_identity(nc, ident[:])
+        nc.vector.memset(ident[:], 0.0)
+        make_identity(nc, ident[:], nomemset=True)
         b_win = [keep.tile([P, 2 * S], F32, name=f"b_win{t}") for t in range(PACK)]
         for t in range(PACK):
             nc.scalar.activation(y_win[t][:, S:], zero[:].to_broadcast([P, S]), ACT.Sigmoid)
@@ -85,10 +87,13 @@ def tile_picked_ccmpclampbhopd_none_po_kernel(
 
         xq_s = keep.tile([P, S], U8, name="xq_s", align_bytes=64)
         nc.vector.tensor_copy(xq_s[:], xs[:].indirect(offs_l[:]))
-        ca_sg = keep.tile([P, S], U8, name="ca_sg", tag="picked_bytes", align_bytes=64)
+        ca_sg = keep.tile([P, S], U8, name="ca_sg", align_bytes=64)
         nc.vector.tensor_copy(ca_sg[:], xs[:].indirect(ca_l[:]))
-        xq_w = keep.tile([P, S], U32, name="xq_w", align_bytes=64)
-        nc.vector.tensor_copy(xq_w[:], xw[:].indirect(offs_l[:]))
+        xq_w = [
+            keep.tile([P, HALF], U32, name="xq_w0", align_bytes=64),
+            shared.tile([P, HALF], U32, name="xq_w1", offset=2560, align_bytes=64),
+        ]
+        nc.vector.tensor_copy(xq_w[0][:], xw[:].indirect(offs_l[:, half_list(0)]))
 
         w_w = keep.tile([P, S], U32, name="w_w", align_bytes=64)
         nc.vector.tensor_copy(
@@ -96,15 +101,14 @@ def tile_picked_ccmpclampbhopd_none_po_kernel(
         )
         w_s = keep.tile([P, S], U8, name="w_s", align_bytes=64)
         nc.vector.tensor_copy(
-            w_s[:].rearrange("p (t m) -> p t m", t=PACK), ws[:].rearrange("p (m t) -> p t m", t=PACK)
+            w_s[:].rearrange("p (t m) -> p t m", t=PACK), ws.rearrange("p (m t) -> p t m", t=PACK)
         )
 
+        nc.vector.tensor_copy(xq_w[1][:], xw[:].indirect(offs_l[:, half_list(1)]))
         ca_w = shared.tile([P, S], U32, name="ca_w", offset=0, align_bytes=64)
         nc.vector.tensor_copy(ca_w[:].rearrange("p (t m) -> p m t", t=PACK), xw[:].indirect(ca_l[:]))
         ca_s = shared.tile([P, S], U8, name="ca_s", offset=2048, align_bytes=64)
         deal_bytes(ca_s, ca_sg)
-        cb_sg = keep.tile([P, S], U8, name="cb_sg", tag="picked_bytes", align_bytes=64)
-        nc.vector.tensor_copy(cb_sg[:], xs[:].indirect(cb_l[:]))
 
         def product(bank, words, scales, t, rhs, rhs_scale):
             cols = slice(t * P, (t + 1) * P)
@@ -120,21 +124,29 @@ def tile_picked_ccmpclampbhopd_none_po_kernel(
 
         y_bank = [psum.tile([P, S], F32, name=f"y_bank{t}", tag=f"yb{t}") for t in range(PACK)]
         sig = keep.tile([P, PACK, S], F32, name="sig")
+        first_bank = psum.tile([P, S], F32, name="first_bank", tag="ab3")
         for t in range(PACK):
-            product(y_bank[t][:], w_w, w_s, t, xq_w[:], xq_s[:])
-            nc.scalar.copy(y_win[t][:, :S], y_bank[t][:])
-            if t == 0:
-                nc.scalar.copy(st_win[t][:, S:], y_bank[t][:])
-            else:
-                nc.vector.tensor_copy(st_win[t][:, S:], y_win[t][:, :S])
+            for h in range(2):
+                cols = half_cols(h)
+                bank = first_bank if t == 0 and h == 0 else y_bank[t]
+                product(bank[:, cols], w_w, w_s, t, xq_w[h][:], xq_s[:, cols])
+                if t == 0:
+                    nc.scalar.copy(y_win[t][:, cols], bank[:, cols])
+                    nc.scalar.copy(st_win[t][:, S + cols.start : S + cols.stop], bank[:, cols])
+            if t > 0:
+                nc.scalar.copy(y_win[t][:, :S], y_bank[t][:])
+                nc.sync.dma_start(st_win[t][:, S:], y_win[t][:, :S])
             nc.vector.tensor_tensor(st_win[t][:, :S], y_win[t][:].indirect(n1_l[:]), st_win[t][:, S:], ALU.subtract)
+            if t == 0:
+                cb_sg = keep.tile([P, S], U8, name="cb_sg", tag="y_win0", align_bytes=64)
+                nc.vector.tensor_copy(cb_sg[:], xs[:].indirect(cb_l[:]))
 
         yg = keep.tile([P, PACK, S], F32, name="yg", tag="y_win3", align_bytes=64)
 
         z_w = keep.tile([P, S], U32, name="z_w", align_bytes=64)
         z_s = keep.tile([P, S], U8, name="z_s", align_bytes=64)
         a_bank = [psum.tile([P, S], F32, name=f"a_bank{t}", tag=f"ab{t}") for t in range(PACK)]
-        a_win = y_win[:1] + st_win[1:]
+        a_win = y_win[1:2] + st_win[1:]
         for t in range(PACK):
             nc.vector.tensor_scalar(yg[:, t, :], st_win[t][:, S:], gs_t[:, t : t + 1], None, ALU.mult)
         for t in range(2):
@@ -152,9 +164,10 @@ def tile_picked_ccmpclampbhopd_none_po_kernel(
                 ALU.mult,
             )
             nc.vector.quantize_mx(z_w[:, cols].bitcast(FP8X4), z_s[:, cols], z_bf[:])
-            product(a_bank[0][:, cols], ca_w, ca_s, 0, z_w[:, cols], z_s[:, cols])
-            nc.scalar.activation(a_win[0][:, cols], a_bank[0][:, cols], ACT.Copy, scale=-0.03125)
-            nc.scalar.activation(b_win[0][:, S + h * HALF : S + (h + 1) * HALF], a_bank[0][:, cols], ACT.Copy, scale=0.0625)
+            bank = psum.tile([P, S], F32, name="first_a_bank", tag="yb3") if h == 0 else a_bank[0]
+            product(bank[:, cols], ca_w, ca_s, 0, z_w[:, cols], z_s[:, cols])
+            nc.scalar.activation(a_win[0][:, cols], bank[:, cols], ACT.Copy, scale=-0.03125)
+            nc.scalar.activation(b_win[0][:, S + h * HALF : S + (h + 1) * HALF], bank[:, cols], ACT.Copy, scale=0.0625)
 
         cb_w = shared.tile([P, S], U32, name="cb_w", offset=4096 + 512, align_bytes=64)
         nc.vector.tensor_copy(cb_w[:].rearrange("p (t m) -> p m t", t=PACK), xw[:].indirect(cb_l[:]))
@@ -171,10 +184,10 @@ def tile_picked_ccmpclampbhopd_none_po_kernel(
         work = ctx.enter_context(tc.tile_pool(name="work", bufs=2))
 
         for t in range(PACK):
-            if t > 0:
-                product(a_bank[t][:], ca_w, ca_s, t, z_w[:], z_s[:])
-                nc.scalar.activation(a_win[t][:, :S], a_bank[t][:], ACT.Copy, scale=-0.03125)
-                nc.scalar.activation(b_win[t][:, S:], a_bank[t][:], ACT.Copy, scale=0.0625)
+            if t + 1 < PACK:
+                product(a_bank[t + 1][:], ca_w, ca_s, t + 1, z_w[:], z_s[:])
+                nc.scalar.activation(a_win[t + 1][:, :S], a_bank[t + 1][:], ACT.Copy, scale=-0.03125)
+                nc.scalar.activation(b_win[t + 1][:, S:], a_bank[t + 1][:], ACT.Copy, scale=0.0625)
             b_bank = psum.tile([P, S], F32, name=f"b_bank{t}", tag=f"yb{t}")
             product(b_bank[:], cb_w, cb_s, t, z_w[:], z_s[:])
             nc.scalar.activation(b_win[t][:, :S], b_bank[:], ACT.Copy, scale=0.0625)
@@ -277,10 +290,9 @@ def tile_picked_ccmpclampbhopd_none_po_kernel(
         fetch_b(b5, n5_l, 1)
         make_low(1)
         interleave(nc.scalar.copy, half_cols(0))
-        planes(half_cols(0))
         finish(1)
-        interleave(nc.vector.tensor_copy, slice(HALF, HALF + 160))
-        interleave(nc.scalar.copy, slice(HALF + 160, S))
+        interleave(nc.vector.tensor_copy, half_cols(1))
+        planes(half_cols(0))
         planes(half_cols(1))
         for q in range(4):
             queue = nc.scalar if q % 2 else nc.sync

@@ -47,11 +47,10 @@ def tile_picked_ccmpclampbhopd_none_po_kernel(
             return slice(h * LIST_COLS // 2, (h + 1) * LIST_COLS // 2)
 
         xs = keep.tile([P, T], U8, name="xs", align_bytes=64)
-        ws_slot = shared.tile([P, 2 * S], U8, name="ws_slot", offset=1984, align_bytes=64)
-        ws = ws_slot[:, :S]
+        ws = keep.tile([P, S], U8, name="ws", tag="ws", align_bytes=64)
         zero = keep.tile([P, 1], F32, name="zero")
         nc.vector.memset(xs[:].bitcast(I32), 0)
-        nc.vector.memset(ws.bitcast(I32), 0)
+        nc.vector.memset(ws[:].bitcast(I32), 0)
         nc.vector.memset(zero[:], 0.0)
 
         ww = keep.tile([P, S], U32, name="ww", tag="ww", align_bytes=64)
@@ -71,7 +70,8 @@ def tile_picked_ccmpclampbhopd_none_po_kernel(
         n4_l = load_list(n4, "n4_l")
         n5_l = load_list(n5, "n5_l")
 
-        y_win = [keep.tile([P, 2 * S], F32, name=f"y_win{t}", tag=f"y_win{t}", align_bytes=64) for t in range(PACK)]
+        y_win = [shared.tile([P, 2 * S], F32, name="y_win0", offset=16384, align_bytes=64)]
+        y_win = y_win + [keep.tile([P, 2 * S], F32, name=f"y_win{t}") for t in range(1, PACK)]
         st_win = [keep.tile([P, 2 * S], F32, name=f"st_win{t}") for t in range(PACK)]
         ident = keep.tile([P, P], F32, name="ident")
         nc.vector.memset(ident[:], 0.0)
@@ -91,7 +91,7 @@ def tile_picked_ccmpclampbhopd_none_po_kernel(
         nc.vector.tensor_copy(ca_sg[:], xs[:].indirect(ca_l[:]))
         xq_w = [
             keep.tile([P, HALF], U32, name="xq_w0", align_bytes=64),
-            shared.tile([P, HALF], U32, name="xq_w1", offset=2560, align_bytes=64),
+            keep.tile([P, HALF], U32, name="xq_w1", align_bytes=64),
         ]
         nc.vector.tensor_copy(xq_w[0][:], xw[:].indirect(offs_l[:, half_list(0)]))
 
@@ -100,14 +100,13 @@ def tile_picked_ccmpclampbhopd_none_po_kernel(
             w_w[:].rearrange("p (t m) -> p m t", t=PACK), ww[:].rearrange("p (m t) -> p m t", t=PACK)
         )
         w_s = keep.tile([P, S], U8, name="w_s", align_bytes=64)
-        nc.vector.tensor_copy(
-            w_s[:].rearrange("p (t m) -> p t m", t=PACK), ws.rearrange("p (m t) -> p t m", t=PACK)
-        )
+        for t in range(PACK):
+            nc.gpsimd.tensor_copy(w_s[:, t * P : (t + 1) * P], ws[:, t::PACK])
 
         nc.vector.tensor_copy(xq_w[1][:], xw[:].indirect(offs_l[:, half_list(1)]))
-        ca_w = shared.tile([P, S], U32, name="ca_w", offset=0, align_bytes=64)
+        ca_w = keep.tile([P, S], U32, name="ca_w", align_bytes=64)
         nc.vector.tensor_copy(ca_w[:].rearrange("p (t m) -> p m t", t=PACK), xw[:].indirect(ca_l[:]))
-        ca_s = shared.tile([P, S], U8, name="ca_s", offset=2048, align_bytes=64)
+        ca_s = keep.tile([P, S], U8, name="ca_s", tag="ws", align_bytes=64)
         deal_bytes(ca_s, ca_sg)
 
         def product(bank, words, scales, t, rhs, rhs_scale):
@@ -138,17 +137,19 @@ def tile_picked_ccmpclampbhopd_none_po_kernel(
                 nc.sync.dma_start(st_win[t][:, S:], y_win[t][:, :S])
             nc.vector.tensor_tensor(st_win[t][:, :S], y_win[t][:].indirect(n1_l[:]), st_win[t][:, S:], ALU.subtract)
             if t == 0:
-                cb_sg = keep.tile([P, S], U8, name="cb_sg", tag="y_win0", align_bytes=64)
+                cb_sg = shared.tile([P, S], U8, name="cb_sg", offset=16384, align_bytes=64)
                 nc.vector.tensor_copy(cb_sg[:], xs[:].indirect(cb_l[:]))
 
-        yg = keep.tile([P, PACK, S], F32, name="yg", tag="y_win3", align_bytes=64)
+        yg = shared.tile([P, PACK, S], F32, name="yg", offset=16384 + 512, align_bytes=64)
 
         z_w = keep.tile([P, S], U32, name="z_w", align_bytes=64)
         z_s = keep.tile([P, S], U8, name="z_s", align_bytes=64)
         a_bank = [psum.tile([P, S], F32, name=f"a_bank{t}", tag=f"ab{t}") for t in range(PACK)]
         a_win = y_win[1:2] + st_win[1:]
-        for t in range(PACK):
-            nc.vector.tensor_scalar(yg[:, t, :], st_win[t][:, S:], gs_t[:, t : t + 1], None, ALU.mult)
+        for t in range(PACK - 1):
+            plain_y = st_win[0][:, S:] if t == 0 else y_win[t][:, :S]
+            nc.gpsimd.tensor_scalar(yg[:, t, :], plain_y, gs_t[:, t : t + 1], 0.0, ALU.mult, ALU.add)
+        nc.vector.tensor_scalar(yg[:, PACK - 1, :], st_win[PACK - 1][:, S:], gs_t[:, PACK - 1 :], None, ALU.mult)
         for t in range(2):
             nc.scalar.activation(sig[:, t, :], st_win[t][:].indirect(n2_l[:]), ACT.Sigmoid)
         for h in range(2):
@@ -166,7 +167,7 @@ def tile_picked_ccmpclampbhopd_none_po_kernel(
             nc.vector.quantize_mx(z_w[:, cols].bitcast(FP8X4), z_s[:, cols], z_bf[:])
             bank = psum.tile([P, S], F32, name="first_a_bank", tag="yb3") if h == 0 else a_bank[0]
             product(bank[:, cols], ca_w, ca_s, 0, z_w[:, cols], z_s[:, cols])
-            nc.scalar.activation(a_win[0][:, cols], bank[:, cols], ACT.Copy, scale=-0.03125)
+            nc.scalar.activation(a_win[0][:, cols], bank[:, cols], ACT.Copy, scale=0.03125)
             nc.scalar.activation(b_win[0][:, S + h * HALF : S + (h + 1) * HALF], bank[:, cols], ACT.Copy, scale=0.0625)
 
         cb_w = shared.tile([P, S], U32, name="cb_w", offset=4096 + 512, align_bytes=64)
@@ -183,14 +184,18 @@ def tile_picked_ccmpclampbhopd_none_po_kernel(
 
         work = ctx.enter_context(tc.tile_pool(name="work", bufs=2))
 
+        b_bank = [psum.tile([P, S], F32, name=f"b_bank{t}", tag=f"yb{t}") for t in range(PACK)]
         for t in range(PACK):
             if t + 1 < PACK:
                 product(a_bank[t + 1][:], ca_w, ca_s, t + 1, z_w[:], z_s[:])
-                nc.scalar.activation(a_win[t + 1][:, :S], a_bank[t + 1][:], ACT.Copy, scale=-0.03125)
-                nc.scalar.activation(b_win[t + 1][:, S:], a_bank[t + 1][:], ACT.Copy, scale=0.0625)
-            b_bank = psum.tile([P, S], F32, name=f"b_bank{t}", tag=f"yb{t}")
-            product(b_bank[:], cb_w, cb_s, t, z_w[:], z_s[:])
-            nc.scalar.activation(b_win[t][:, :S], b_bank[:], ACT.Copy, scale=0.0625)
+            product(b_bank[t][:], cb_w, cb_s, t, z_w[:], z_s[:])
+
+        def take_a(t):
+            nc.scalar.activation(a_win[t][:, :S], a_bank[t][:], ACT.Copy, scale=0.03125 if t < 2 else -0.03125)
+            nc.scalar.activation(b_win[t][:, S:], a_bank[t][:], ACT.Copy, scale=0.0625)
+
+        def take_b(t):
+            nc.scalar.activation(b_win[t][:, :S], b_bank[t][:], ACT.Copy, scale=0.0625)
 
         def interleave(copy, cols):
             copy(
@@ -209,18 +214,18 @@ def tile_picked_ccmpclampbhopd_none_po_kernel(
         d4 = [None] * last
         d5 = [None] * last
         turned = {}
-        spans = {0: [slice(0, S)], 1: [slice(0, S)], 2: [half_cols(0), half_cols(1)]}
+        spans = {2: [half_cols(0), half_cols(1)]}
 
         def blocks(cols):
             return [slice(c, c + P) for c in range(cols.start, cols.stop, P)]
 
         def make_u(t):
             u[t] = keep.tile([P, S], F32, name=f"u{t}", tag=f"u{t}")
-            nc.vector.tensor_tensor(u[t][:], a_win[t][:].indirect(n3_l[:]), b_win[t][:, S:], ALU.add)
+            nc.vector.tensor_tensor(u[t][:], a_win[t][:].indirect(n3_l[:]), b_win[t][:, S:], ALU.subtract if t < 2 else ALU.add)
 
         def turn_u(t):
             for i, cols in enumerate(spans[t]):
-                turned[t, i] = psum.tile([P, S], F32, name=f"turned{t}_{i}", tag=f"ab{t}" if i == 0 else "ab0")
+                turned[t, i] = psum.tile([P, S], F32, name=f"turned{t}_{i}", tag="yb1" if i == 0 else "ab1")
                 for block in blocks(cols):
                     nc.tensor.matmul(
                         turned[t, i][:, block], u[t][:, block], ident[:],
@@ -229,7 +234,7 @@ def tile_picked_ccmpclampbhopd_none_po_kernel(
 
         def make_d4(t):
             d4[t] = keep.tile([P, S], F32, name=f"d4_{t}", tag=f"u{last}" if t == last - 1 else f"d4_{t}")
-            nc.vector.tensor_tensor(d4[t][:], b_win[t][:].indirect(n4_l[:]), u[t][:], ALU.subtract)
+            nc.vector.tensor_tensor(d4[t][:], b_win[t][:].indirect(n4_l[:]), u[t][:], ALU.add if t < 2 else ALU.subtract)
 
         def make_d5(t):
             d5[t] = keep.tile([P, S], F32, name=f"d5_{t}")
@@ -247,11 +252,45 @@ def tile_picked_ccmpclampbhopd_none_po_kernel(
                         start=False, stop=block.stop == cols.stop, is_transpose=True,
                     )
                 nc.scalar.copy(turned_sb[:, cols], turned[t, i][:, cols])
+            turn_back(1)
             for i, cols in enumerate(spans[t]):
-                back = psum.tile([P, S], F32, name=f"back{t}_{i}", tag=f"yb{t}" if i == 0 else "yb0")
+                back = psum.tile([P, S], F32, name=f"back{t}_{i}", tag="yb3" if i == 0 else "yb0")
                 for block in blocks(cols):
                     nc.tensor.transpose(back[:, block], turned_sb[:, block], ident[:])
                 nc.scalar.copy(res[:, t, cols], back[:, cols])
+            nc.sync.dma_start(out_rows[:, t, :], res[:, t, :])
+
+        r4 = [keep.tile([P, S], F32, name=f"r4_{t}") for t in range(2)]
+        g5 = [keep.tile([P, S], F32, name=f"g5_{t}") for t in range(2)]
+        m_turned = [keep.tile([P, S], F32, name=f"m_turned{t}") for t in range(2)]
+        e_turned = [keep.tile([P, S], F32, name=f"e_turned{t}") for t in range(2)]
+
+        def turned_sum(tag, first, second):
+            bank = psum.tile([P, S], F32, name="sum_bank", tag=tag)
+            for src in (first, second):
+                for block in blocks(slice(0, S)):
+                    nc.tensor.matmul(
+                        bank[:, block], src[:, block], ident[:],
+                        start=src is first and block.start == 0,
+                        stop=src is second and block.stop == S,
+                        is_transpose=True,
+                    )
+            return bank
+
+        def make_r4(t):
+            nc.scalar.activation(r4[t][:], d4[t][:], ACT.Relu, scale=-1.0)
+
+        def make_g5(t):
+            nc.vector.tensor_tensor(g5[t][:], b_win[t][:].indirect(n5_l[:]), r4[t][:], ALU.add)
+
+        def turn_m(t):
+            nc.scalar.activation(m_turned[t][:], turned_sum(f"yb{t}", u[t], r4[t])[:], ACT.Copy, scale=-1.0)
+
+        def turn_e(t):
+            nc.scalar.activation(e_turned[t][:], turned_sum(f"ab{t}", u[t], g5[t])[:], ACT.Relu)
+
+        def turn_back(t):
+            nc.scalar.copy(res[:, t, :], turned_sum("ab2" if t == 0 else "yb2", m_turned[t], e_turned[t])[:])
             nc.sync.dma_start(out_rows[:, t, :], res[:, t, :])
 
         b4 = [keep.tile([P, HALF], F32, name=f"b4_{h}") for h in range(2)]
@@ -270,16 +309,28 @@ def tile_picked_ccmpclampbhopd_none_po_kernel(
             nc.sync.dma_start(out_rows[:, last, cols], res[:, last, cols])
 
         make_u(0)
+        take_a(1)
         make_u(1)
+        take_b(0)
         make_d4(0)
-        make_d5(0)
-        make_u(2)
-        clamp_and_add(0)
+        take_b(1)
         make_d4(1)
-        make_d5(1)
+        take_a(2)
+        make_r4(0)
+        make_g5(0)
+        take_b(2)
+        make_r4(1)
+        make_u(2)
+        make_g5(1)
+        turn_m(0)
+        take_a(3)
+        turn_e(0)
+        take_b(3)
         make_d4(2)
-        clamp_and_add(1)
         make_d5(2)
+        turn_m(1)
+        turn_back(0)
+        turn_e(1)
         fetch_b(b4, n4_l, 0)
         clamp_and_add(2)
         make_u(last)

from contextlib import ExitStack

import concourse.mybir as mybir
from concourse.masks import make_identity

F32 = mybir.dt.float32
BF16 = mybir.dt.bfloat16
I32 = mybir.dt.int32
U32 = mybir.dt.uint32
U16 = mybir.dt.uint16
U8 = mybir.dt.uint8
FP8X4 = mybir.dt.float8_e4m3fn_x4
ALU = mybir.AluOpType
ACT = mybir.ActivationFunctionType

P = 128
PACK = 4
T = 2048
S = 512
HALF = S // 2
LIST_COLS = S // 16
FLOPS = 3 * 2 * 512 * 512 * 512


def tile_picked_ccmpclampbhopd_none_po_kernel(
    tc, x_words, x_scales, w1_words, w1_scales, gs, offs, n1, n2, ca, cb, n3, n4, n5, out_0, out_1, out_2
):
    nc = tc.nc
    with ExitStack() as ctx:
        keep = ctx.enter_context(tc.tile_pool(name="keep", bufs=1))
        shared = ctx.enter_context(tc.tile_pool(name="shared", bufs=1))
        psum = ctx.enter_context(tc.psum_pool(name="psum", bufs=1))

        def load_list(src, name):
            tile = keep.tile([P, LIST_COLS], U16, name=name)
            nc.sync.dma_start(tile[:], src)
            return tile

        def load_scale_rows(queue, tile, src):
            for q in range(4):
                queue.dma_start(tile[32 * q : 32 * q + 4, :].bitcast(I32), src[0, 4 * q : 4 * q + 4, :].bitcast(I32))

        def half_cols(h):
            return slice(h * HALF, (h + 1) * HALF)

        def half_list(h):
            return slice(h * LIST_COLS // 2, (h + 1) * LIST_COLS // 2)

        xs = keep.tile([P, T], U8, name="xs", align_bytes=64)
        ws = keep.tile([P, S], U8, name="ws", tag="ws", align_bytes=64)
        zero = keep.tile([P, 1], F32, name="zero")
        nc.vector.memset(xs[:].bitcast(I32), 0)
        nc.vector.memset(ws[:].bitcast(I32), 0)
        nc.vector.memset(zero[:], 0.0)

        ww = keep.tile([P, S], U32, name="ww", tag="ww", align_bytes=64)
        nc.sync.dma_start(ww[:].bitcast(I32), w1_words[0].rearrange("p n t -> p (n t)").bitcast(I32))
        offs_l = load_list(offs, "offs_l")
        ca_l = load_list(ca, "ca_l")
        load_scale_rows(nc.sync, xs, x_scales)
        xw = keep.tile([P, T], U32, name="xw", align_bytes=64)
        nc.sync.dma_start(xw[:].bitcast(I32), x_words[0].rearrange("p n t -> p (n t)").bitcast(I32))
        load_scale_rows(nc.sync, ws, w1_scales)
        n1_l = load_list(n1, "n1_l")
        gs_t = keep.tile([P, PACK], F32, name="gs_t")
        nc.sync.dma_start(gs_t[:], gs.rearrange("(p t) o -> p (t o)", t=PACK))
        cb_l = load_list(cb, "cb_l")
        n2_l = load_list(n2, "n2_l")
        n3_l = load_list(n3, "n3_l")
        n4_l = load_list(n4, "n4_l")
        n5_l = load_list(n5, "n5_l")

        y_win = [shared.tile([P, 2 * S], F32, name="y_win0", offset=16384, align_bytes=64)]
        y_win = y_win + [keep.tile([P, 2 * S], F32, name=f"y_win{t}") for t in range(1, PACK)]
        st_win = [keep.tile([P, 2 * S], F32, name=f"st_win{t}") for t in range(PACK)]
        ident = keep.tile([P, P], F32, name="ident")
        nc.vector.memset(ident[:], 0.0)
        make_identity(nc, ident[:], nomemset=True)
        b_win = [keep.tile([P, 2 * S], F32, name=f"b_win{t}") for t in range(PACK)]
        for t in range(PACK):
            nc.scalar.activation(y_win[t][:, S:], zero[:].to_broadcast([P, S]), ACT.Sigmoid)

        def deal_bytes(dealt, src):
            nc.vector.tensor_copy(
                dealt[:].rearrange("p (t m) -> p t m", t=PACK), src[:].rearrange("p (m t) -> p t m", t=PACK)
            )

        xq_s = keep.tile([P, S], U8, name="xq_s", align_bytes=64)
        nc.vector.tensor_copy(xq_s[:], xs[:].indirect(offs_l[:]))
        ca_sg = keep.tile([P, S], U8, name="ca_sg", align_bytes=64)
        nc.vector.tensor_copy(ca_sg[:], xs[:].indirect(ca_l[:]))
        xq_w = [
            keep.tile([P, HALF], U32, name="xq_w0", align_bytes=64),
            keep.tile([P, HALF], U32, name="xq_w1", align_bytes=64),
        ]
        nc.vector.tensor_copy(xq_w[0][:], xw[:].indirect(offs_l[:, half_list(0)]))

        w_w = keep.tile([P, S], U32, name="w_w", align_bytes=64)
        nc.vector.tensor_copy(
            w_w[:].rearrange("p (t m) -> p m t", t=PACK), ww[:].rearrange("p (m t) -> p m t", t=PACK)
        )
        w_s = keep.tile([P, S], U8, name="w_s", align_bytes=64)
        for t in range(PACK):
            nc.gpsimd.tensor_copy(w_s[:, t * P : (t + 1) * P], ws[:, t::PACK])

        nc.vector.tensor_copy(xq_w[1][:], xw[:].indirect(offs_l[:, half_list(1)]))
        ca_w = keep.tile([P, S], U32, name="ca_w", align_bytes=64)
        nc.vector.tensor_copy(ca_w[:].rearrange("p (t m) -> p m t", t=PACK), xw[:].indirect(ca_l[:]))
        ca_s = keep.tile([P, S], U8, name="ca_s", tag="ws", align_bytes=64)
        deal_bytes(ca_s, ca_sg)

        def product(bank, words, scales, t, rhs, rhs_scale):
            cols = slice(t * P, (t + 1) * P)
            nc.tensor.matmul_mx(
                out=bank,
                lhsT=words[:, cols].bitcast(FP8X4),
                lhsT_scale=scales[:, cols],
                rhs=rhs.bitcast(FP8X4),
                rhs_scale=rhs_scale,
                start=True,
                stop=True,
            )

        y_bank = [psum.tile([P, S], F32, name=f"y_bank{t}", tag=f"yb{t}") for t in range(PACK)]
        sig = keep.tile([P, PACK, S], F32, name="sig")
        first_bank = psum.tile([P, S], F32, name="first_bank", tag="ab3")
        for t in range(PACK):
            for h in range(2):
                cols = half_cols(h)
                bank = first_bank if t == 0 and h == 0 else y_bank[t]
                product(bank[:, cols], w_w, w_s, t, xq_w[h][:], xq_s[:, cols])
                if t == 0:
                    nc.scalar.copy(y_win[t][:, cols], bank[:, cols])
                    nc.scalar.copy(st_win[t][:, S + cols.start : S + cols.stop], bank[:, cols])
            if t > 0:
                nc.scalar.copy(y_win[t][:, :S], y_bank[t][:])
                nc.sync.dma_start(st_win[t][:, S:], y_win[t][:, :S])
            nc.vector.tensor_tensor(st_win[t][:, :S], y_win[t][:].indirect(n1_l[:]), st_win[t][:, S:], ALU.subtract)
            if t == 0:
                cb_sg = shared.tile([P, S], U8, name="cb_sg", offset=16384, align_bytes=64)
                nc.vector.tensor_copy(cb_sg[:], xs[:].indirect(cb_l[:]))

        yg = shared.tile([P, PACK, S], F32, name="yg", offset=16384 + 512, align_bytes=64)

        z_w = keep.tile([P, S], U32, name="z_w", align_bytes=64)
        z_s = keep.tile([P, S], U8, name="z_s", align_bytes=64)
        a_bank = [psum.tile([P, S], F32, name=f"a_bank{t}", tag=f"ab{t}") for t in range(PACK)]
        a_win = y_win[1:2] + st_win[1:]
        for t in range(PACK - 1):
            plain_y = st_win[0][:, S:] if t == 0 else y_win[t][:, :S]
            nc.gpsimd.tensor_scalar(yg[:, t, :], plain_y, gs_t[:, t : t + 1], 0.0, ALU.mult, ALU.add)
        nc.vector.tensor_scalar(yg[:, PACK - 1, :], st_win[PACK - 1][:, S:], gs_t[:, PACK - 1 :], None, ALU.mult)
        for t in range(2):
            nc.scalar.activation(sig[:, t, :], st_win[t][:].indirect(n2_l[:]), ACT.Sigmoid)
        for h in range(2):
            for t in range(2, PACK):
                nc.scalar.activation(sig[:, t, half_cols(h)], st_win[t][:].indirect(n2_l[:, half_list(h)]), ACT.Sigmoid)
        for h in range(2):
            cols = half_cols(h)
            z_bf = shared.tile([P, HALF * PACK], BF16, name=f"z_bf{h}", offset=8192 if h == 0 else 4096 + 256, align_bytes=64)
            nc.vector.tensor_tensor(
                z_bf[:].rearrange("p (c i t) -> p c t i", i=4, t=PACK),
                yg[:, :, cols].rearrange("p t (c i) -> p c t i", i=4),
                sig[:, :, cols].rearrange("p t (c i) -> p c t i", i=4),
                ALU.mult,
            )
            nc.vector.quantize_mx(z_w[:, cols].bitcast(FP8X4), z_s[:, cols], z_bf[:])
            bank = psum.tile([P, S], F32, name="first_a_bank", tag="yb3") if h == 0 else a_bank[0]
            product(bank[:, cols], ca_w, ca_s, 0, z_w[:, cols], z_s[:, cols])
            nc.scalar.activation(a_win[0][:, cols], bank[:, cols], ACT.Copy, scale=0.03125)
            nc.scalar.activation(b_win[0][:, S + h * HALF : S + (h + 1) * HALF], bank[:, cols], ACT.Copy, scale=0.0625)

        cb_w = shared.tile([P, S], U32, name="cb_w", offset=4096 + 512, align_bytes=64)
        nc.vector.tensor_copy(cb_w[:].rearrange("p (t m) -> p m t", t=PACK), xw[:].indirect(cb_l[:]))
        cb_s = shared.tile([P, S], U8, name="cb_s", offset=4096, align_bytes=64)
        deal_bytes(cb_s, cb_sg)

        res = keep.tile([P, PACK, S], F32, name="res")
        out_rows = out_0.rearrange("(p t) s -> p t s", t=PACK)
        o_w = keep.tile([P, S], U32, name="o_w", align_bytes=64)
        o_s = keep.tile([P, S], U8, name="o_s", align_bytes=64)
        o_bf = keep.tile([P, S * PACK], BF16, name="o_bf", align_bytes=64)
        out_words = out_1[0].rearrange("p n t -> p (n t)").bitcast(I32)

        work = ctx.enter_context(tc.tile_pool(name="work", bufs=2))

        b_bank = [psum.tile([P, S], F32, name=f"b_bank{t}", tag=f"yb{t}") for t in range(PACK)]
        for t in range(PACK):
            if t + 1 < PACK:
                product(a_bank[t + 1][:], ca_w, ca_s, t + 1, z_w[:], z_s[:])
            product(b_bank[t][:], cb_w, cb_s, t, z_w[:], z_s[:])

        def take_a(t):
            nc.scalar.activation(a_win[t][:, :S], a_bank[t][:], ACT.Copy, scale=0.03125 if t < 2 else -0.03125)
            nc.scalar.activation(b_win[t][:, S:], a_bank[t][:], ACT.Copy, scale=0.0625)

        def take_b(t):
            nc.scalar.activation(b_win[t][:, :S], b_bank[t][:], ACT.Copy, scale=0.0625)

        def interleave(copy, cols):
            copy(
                o_bf[:, cols.start * PACK : cols.stop * PACK].rearrange("p (c i t) -> p c t i", i=4, t=PACK),
                res[:, :, cols].rearrange("p t (c i) -> p c t i", i=4),
            )

        def planes(cols):
            nc.vector.quantize_mx(
                o_w[:, cols].bitcast(FP8X4), o_s[:, cols], o_bf[:, cols.start * PACK : cols.stop * PACK]
            )
            nc.sync.dma_start(out_words[:, cols], o_w[:, cols].bitcast(I32))

        last = PACK - 1
        u = [None] * PACK
        d4 = [None] * last
        d5 = [None] * last
        turned = {}
        spans = {2: [half_cols(0), half_cols(1)]}

        def blocks(cols):
            return [slice(c, c + P) for c in range(cols.start, cols.stop, P)]

        def make_u(t):
            u[t] = keep.tile([P, S], F32, name=f"u{t}", tag=f"u{t}")
            nc.vector.tensor_tensor(u[t][:], a_win[t][:].indirect(n3_l[:]), b_win[t][:, S:], ALU.subtract if t < 2 else ALU.add)

        def turn_u(t):
            for i, cols in enumerate(spans[t]):
                turned[t, i] = psum.tile([P, S], F32, name=f"turned{t}_{i}", tag="yb1" if i == 0 else "ab1")
                for block in blocks(cols):
                    nc.tensor.matmul(
                        turned[t, i][:, block], u[t][:, block], ident[:],
                        start=block.start == cols.start, stop=False, is_transpose=True,
                    )

        def make_d4(t):
            d4[t] = keep.tile([P, S], F32, name=f"d4_{t}", tag=f"u{last}" if t == last - 1 else f"d4_{t}")
            nc.vector.tensor_tensor(d4[t][:], b_win[t][:].indirect(n4_l[:]), u[t][:], ALU.add if t < 2 else ALU.subtract)

        def make_d5(t):
            d5[t] = keep.tile([P, S], F32, name=f"d5_{t}")
            nc.vector.tensor_tensor(d5[t][:], b_win[t][:].indirect(n5_l[:]), u[t][:], ALU.subtract)

        def clamp_and_add(t):
            w = work.tile([P, S], F32, name="w")
            nc.vector.scalar_tensor_tensor(w[:], d4[t][:], 0.0, d5[t][:], ALU.min, ALU.max)
            turn_u(t)
            turned_sb = work.tile([P, S], F32, name="turned_sb")
            for i, cols in enumerate(spans[t]):
                for block in blocks(cols):
                    nc.tensor.matmul(
                        turned[t, i][:, block], w[:, block], ident[:],
                        start=False, stop=block.stop == cols.stop, is_transpose=True,
                    )
                nc.scalar.copy(turned_sb[:, cols], turned[t, i][:, cols])
            turn_back(1)
            for i, cols in enumerate(spans[t]):
                back = psum.tile([P, S], F32, name=f"back{t}_{i}", tag="yb3" if i == 0 else "yb0")
                for block in blocks(cols):
                    nc.tensor.transpose(back[:, block], turned_sb[:, block], ident[:])
                nc.scalar.copy(res[:, t, cols], back[:, cols])
            nc.sync.dma_start(out_rows[:, t, :], res[:, t, :])

        r4 = [keep.tile([P, S], F32, name=f"r4_{t}") for t in range(2)]
        g5 = [keep.tile([P, S], F32, name=f"g5_{t}") for t in range(2)]
        m_turned = [keep.tile([P, S], F32, name=f"m_turned{t}") for t in range(2)]
        e_turned = [keep.tile([P, S], F32, name=f"e_turned{t}") for t in range(2)]

        def turned_sum(tag, first, second):
            bank = psum.tile([P, S], F32, name="sum_bank", tag=tag)
            for src in (first, second):
                for block in blocks(slice(0, S)):
                    nc.tensor.matmul(
                        bank[:, block], src[:, block], ident[:],
                        start=src is first and block.start == 0,
                        stop=src is second and block.stop == S,
                        is_transpose=True,
                    )
            return bank

        def make_r4(t):
            nc.scalar.activation(r4[t][:], d4[t][:], ACT.Relu, scale=-1.0)

        def make_g5(t):
            nc.vector.tensor_tensor(g5[t][:], b_win[t][:].indirect(n5_l[:]), r4[t][:], ALU.add)

        def turn_m(t):
            nc.scalar.activation(m_turned[t][:], turned_sum(f"yb{t}", u[t], r4[t])[:], ACT.Copy, scale=-1.0)

        def turn_e(t):
            nc.scalar.activation(e_turned[t][:], turned_sum(f"ab{t}", u[t], g5[t])[:], ACT.Relu)

        def turn_back(t):
            nc.scalar.copy(res[:, t, :], turned_sum("ab2" if t == 0 else "yb2", m_turned[t], e_turned[t])[:])
            nc.sync.dma_start(out_rows[:, t, :], res[:, t, :])

        b4 = [keep.tile([P, HALF], F32, name=f"b4_{h}") for h in range(2)]
        b5 = [keep.tile([P, HALF], F32, name=f"b5_{h}") for h in range(2)]
        low = [keep.tile([P, HALF], F32, name=f"low{h}") for h in range(2)]

        def fetch_b(dst, lst, h):
            nc.vector.tensor_copy(dst[h][:], b_win[last][:].indirect(lst[:, half_list(h)]))

        def make_low(h):
            nc.vector.tensor_tensor(low[h][:], u[last][:, half_cols(h)], b4[h][:], ALU.min)

        def finish(h):
            cols = half_cols(h)
            nc.vector.tensor_tensor(res[:, last, cols], low[h][:], b5[h][:], ALU.max)
            nc.sync.dma_start(out_rows[:, last, cols], res[:, last, cols])

        make_u(0)
        take_a(1)
        make_u(1)
        take_b(0)
        make_d4(0)
        take_b(1)
        make_d4(1)
        take_a(2)
        make_r4(0)
        make_g5(0)
        take_b(2)
        make_r4(1)
        make_u(2)
        make_g5(1)
        turn_m(0)
        take_a(3)
        turn_e(0)
        take_b(3)
        make_d4(2)
        make_d5(2)
        turn_m(1)
        turn_back(0)
        turn_e(1)
        fetch_b(b4, n4_l, 0)
        clamp_and_add(2)
        make_u(last)
        fetch_b(b5, n5_l, 0)
        make_low(0)
        fetch_b(b4, n4_l, 1)
        finish(0)
        fetch_b(b5, n5_l, 1)
        make_low(1)
        interleave(nc.scalar.copy, half_cols(0))
        finish(1)
        interleave(nc.vector.tensor_copy, half_cols(1))
        planes(half_cols(0))
        planes(half_cols(1))
        for q in range(4):
            queue = nc.scalar if q % 2 else nc.sync
            queue.dma_start(out_2[0, 4 * q : 4 * q + 4, :].bitcast(I32), o_s[32 * q : 32 * q + 4, :].bitcast(I32))
